import numpy as np
import ml_dtypes


def mxq(x, axis, fmt="e4m3"):
    dtype, down = {"e4m3": (ml_dtypes.float8_e4m3fn, 7), "e5m2": (ml_dtypes.float8_e5m2, 14)}[fmt]
    v = np.moveaxis(np.asarray(x, np.float32).astype(ml_dtypes.bfloat16).astype(np.float64), axis, -1)
    blocks = v.reshape(v.shape[:-1] + (-1, 32))
    amax = np.abs(blocks).max(-1, keepdims=True)
    byte = np.maximum(np.where(amax > 0, np.frexp(amax)[1] - 1 + 127, 0) - down, 1)
    scale = np.exp2(byte - 127.0)
    codes = (blocks / scale).astype(np.float32).astype(dtype).astype(np.float64)
    return np.moveaxis((codes * scale).reshape(v.shape), -1, axis)


WIDE = False


def mx_kscale(k):
    if not WIDE:
        return np.ones(k)
    levels = np.array([10, -10, 5, -5, 0])
    if k % 512:
        return np.exp2(np.random.permutation(np.resize(levels, k // 32))).repeat(32)
    a = np.empty((k // 512, 16))
    for p in range(k // 512):
        a[p, :8] = np.random.permutation(np.resize(levels, 8))
        for g in range(8):
            far = levels[np.abs(levels - a[p, g]) >= 10]
            a[p, g + 8] = far[np.random.randint(len(far))]
    return np.exp2(a.ravel()).repeat(32)


def f64(x):
    return np.asarray(x).astype(np.float64)


def striped(idx):
    return np.tile(idx.reshape(-1, 16).T, (8, 1)).astype(np.uint16)


def unstriped(offs):
    return offs[:16].T.reshape(-1).astype(np.int64)


def striped8(idx):
    return np.concatenate([x.reshape(-1, 16).T for x in idx]).astype(np.uint16)


def runs(offs, k):
    lists = np.stack([offs[16 * r : 16 * r + 16].T.reshape(-1) for r in range(8)]).astype(np.int64)
    return lists[np.arange(k) % 512 // 64]


def pack_weight(w):
    k, n = w.shape
    w = f64(np.asarray(w, np.float32).astype(ml_dtypes.bfloat16)).reshape(k // 32, 32, n)
    amax = np.abs(w).max(1)
    byte = np.clip(np.where(amax > 0, np.frexp(amax)[1] - 1 + 127 - 7, 1), 1, 254)
    scaled = (w * np.exp2(127.0 - byte)[:, None, :]).reshape(k, n).astype(np.float32)
    words = np.ascontiguousarray(scaled.reshape(k // 512, 128, 4, n).transpose(0, 1, 3, 2)).astype(ml_dtypes.float8_e4m3fn).view(np.uint8)
    return words, np.ascontiguousarray(byte.astype(np.uint8).reshape(k // 512, 16, n))


def unpack_weight(words, scales):
    g, p, n, _ = words.shape
    vals = np.ascontiguousarray(words).view(ml_dtypes.float8_e4m3fn).astype(np.float64) * np.repeat(np.exp2(scales.astype(np.float64) - 127.0), 8, axis=1)[..., None]
    return vals.transpose(0, 1, 3, 2).reshape(g * 512, n)


def relu(v):
    return np.maximum(v, 0.0)


def sigmoid(v):
    return 1.0 / (1.0 + np.exp(-np.maximum(v, -700.0)))

def planes(y):
    n, m = y.shape
    v = y.astype(np.float32).astype(ml_dtypes.bfloat16).astype(np.float64).reshape(n // 32, 32, m)
    top = np.abs(v).max(1)
    byte = np.clip(np.where(top > 0, np.frexp(top)[1] - 1 + 127 - 7, 1), 1, 254)
    codes = (v * np.exp2(127.0 - byte)[:, None, :]).reshape(n, m).astype(np.float32).astype(ml_dtypes.float8_e4m3fn).view(np.uint8)
    words = codes.reshape(n // 512, 128, 4, m).transpose(0, 1, 3, 2)
    return np.ascontiguousarray(words), np.ascontiguousarray(byte.astype(np.uint8).reshape(n // 512, 16, m))


K, T, S, N, H = 512, 2048, 256, 512, 512


def setup_inputs():
    n = np.random.standard_normal
    s = mx_kscale(K)[:, None]
    u = mx_kscale(H)
    packed_xT = pack_weight(n((K, T)) * s)
    packed_w1 = pack_weight(n((K, H)) / np.sqrt(K) / s)
    packed_w2 = pack_weight(n((K, H)) / np.sqrt(K) / s)
    packed_w3 = pack_weight(n((H, N)) / np.sqrt(H) / u[:, None])
    return {
        "x_words": packed_xT[0],
        "x_scales": packed_xT[1],
        "w1_words": packed_w1[0],
        "w1_scales": packed_w1[1],
        "w2_words": packed_w2[0],
        "w2_scales": packed_w2[1],
        "sl": np.random.uniform(1.0, 2.0, (H, 1)).astype(np.float32),
        "th": (0.5 * n((H, 1))).astype(np.float32),
        "sl2": np.random.uniform(1.0, 2.0, (H, 1)).astype(np.float32),
        "th2": (0.5 * n((H, 1))).astype(np.float32),
        "gn": (np.random.uniform(0.5, 1.5, (H, 1)) * u[:, None]).astype(np.float32),
        "w3_words": packed_w3[0],
        "w3_scales": packed_w3[1],
        "offs": striped(np.random.permutation(T)[:S]),
        "two": striped(np.random.permutation(T)[:S]),
        "n1": striped(np.random.permutation(S)),
        "n2": striped(np.random.permutation(S)),
        "n3": striped8(np.stack([np.random.permutation(S) for _ in range(8)])),
        "n4": striped8(np.stack([np.random.permutation(S) for _ in range(8)])),
    }


def reference(x_words, x_scales, w1_words, w1_scales, w2_words, w2_scales, sl, th, sl2, th2, gn, w3_words, w3_scales, offs, two, n1, n2, n3, n4):
    xq = unpack_weight(x_words, x_scales)[:, unstriped(offs)]
    y = unpack_weight(w1_words, w1_scales).T @ xq
    sg = sigmoid(f64(sl) * (y[:, unstriped(n1)] - f64(th)))
    x_two = unpack_weight(x_words, x_scales)[:, unstriped(two)]
    d = unpack_weight(w2_words, w2_scales).T @ x_two
    sg2 = sigmoid(f64(sl2) * (d[:, unstriped(n2)] - f64(th2)))
    z = f64(gn) * (sg * d + sg2 * y)
    h = unpack_weight(w3_words, w3_scales).T @ mxq(z, 0, "e4m3")
    out_0 = relu(h - (h[np.arange(N)[:, None], runs(n3, N)])) + 0.5 * (relu(h[np.arange(N)[:, None], runs(n4, N)] - h))
    return (out_0,) + planes(out_0)

@@ -1,0 +1,276 @@
+from contextlib import ExitStack
+
+import concourse.mybir as mybir
+
+K, T, S, N, H = 512, 2048, 256, 512, 512
+FLOPS = 2 * K * H * S * 2 + 2 * H * N * S
+
+F32 = mybir.dt.float32
+BF16 = mybir.dt.bfloat16
+I32 = mybir.dt.int32
+U32 = mybir.dt.uint32
+U16 = mybir.dt.uint16
+U8 = mybir.dt.uint8
+FP8X4 = mybir.dt.float8_e4m3fn_x4
+ALU = mybir.AluOpType
+ACT = mybir.ActivationFunctionType
+
+P = 128
+PACK = 4
+HALF = S // 2
+WHOLE = (0, 1)
+
+
+def tile_picked_twlcxbhinge_none_po_kernel(
+    tc, x_words, x_scales, w1_words, w1_scales, w2_words, w2_scales, sl, th, sl2, th2, gn, w3_words, w3_scales,
+    offs, two, n1, n2, n3, n4, out_0, out_1, out_2,
+):
+    nc = tc.nc
+    with ExitStack() as ctx:
+        keep = ctx.enter_context(tc.tile_pool(name="keep", bufs=1))
+        psum = ctx.enter_context(tc.psum_pool(name="psum", bufs=1))
+
+        def sb(name, shape, dtype):
+            return keep.tile(shape, dtype, name=name, align_bytes=64)
+
+        def load_list(name, source):
+            tile = keep.tile([P, S // 16], U16, name=name)
+            nc.sync.dma_start(tile[:], source)
+            return tile
+
+        def load_words(name, source, width):
+            tile = sb(name, [P, width], U32)
+            nc.sync.dma_start(tile[:].bitcast(I32), source[0].rearrange("p n t -> p (n t)").bitcast(I32))
+            return tile
+
+        def zeroed(name, width, engine):
+            tile = sb(name, [P, width], U8)
+            engine.memset(tile[:].bitcast(I32), 0)
+            return tile
+
+        def load_scale_rows(tile, source, queues):
+            for q in range(4):
+                queues[q].dma_start(tile[32 * q : 32 * q + 4, :].bitcast(I32), source[0, 4 * q : 4 * q + 4, :].bitcast(I32))
+
+        def load_rows(name, source, queue):
+            tile = sb(name, [P, PACK], F32)
+            queue.dma_start(tile[:], source.rearrange("(p t) o -> p (t o)", t=PACK))
+            return tile
+
+        def deal(name, raw, dtype, run, engine):
+            dealt = sb(name, [P, PACK, P], dtype)
+            engine.tensor_copy(
+                dealt[:].rearrange("p t (a i) -> p a t i", i=run),
+                raw[:].rearrange("p (a i t) -> p a t i", i=run, t=PACK),
+            )
+            return dealt
+
+        def cols(half):
+            return slice(half * HALF, (half + 1) * HALF)
+
+        def offsets(lst, c):
+            return lst[:, c.start // 16 : c.stop // 16]
+
+        def window(name, t):
+            if t not in WHOLE:
+                return sb(name, [P, S], F32)
+            tile = sb(name, [P, 2 * S], F32)
+            nc.vector.memset(tile[:, S:], 0.0)
+            return tile
+
+        xs = zeroed("xs", T, nc.vector)
+        w1s_raw = zeroed("w1s_raw", H, nc.gpsimd)
+        w2s_raw = zeroed("w2s_raw", H, nc.vector)
+        w3s_raw = zeroed("w3s_raw", N, nc.vector)
+
+        offs_t = load_list("offs_t", offs)
+        w1_raw = load_words("w1_raw", w1_words, H)
+        xw = load_words("xw", x_words, T)
+        load_scale_rows(w1s_raw, w1_scales, [nc.gpsimd, nc.gpsimd, nc.gpsimd, nc.scalar])
+        load_scale_rows(xs, x_scales, [nc.scalar] * 4)
+        two_t = load_list("two_t", two)
+        w2_raw = load_words("w2_raw", w2_words, H)
+        load_scale_rows(w2s_raw, w2_scales, [nc.scalar] * 4)
+        n1_t = load_list("n1_t", n1)
+        sl_t = load_rows("sl_t", sl, nc.sync)
+        th_t = load_rows("th_t", th, nc.sync)
+        n2_t = load_list("n2_t", n2)
+        sl2_t = load_rows("sl2_t", sl2, nc.sync)
+        th2_t = load_rows("th2_t", th2, nc.sync)
+        gn_t = load_rows("gn_t", gn, nc.sync)
+        w3_raw = load_words("w3_raw", w3_words, N)
+        load_scale_rows(w3s_raw, w3_scales, [nc.sync] * 4)
+        n3_t = load_list("n3_t", n3)
+        n4_t = load_list("n4_t", n4)
+
+        w1 = deal("w1", w1_raw, U32, 4, nc.vector)
+        w1s = deal("w1s", w1s_raw, U8, 16, nc.vector)
+        w2s = deal("w2s", w2s_raw, U8, 16, nc.vector)
+
+        def bias(name, slope, threshold):
+            product = sb(name + "_product", [P, PACK], F32)
+            nc.gpsimd.tensor_tensor(product[:], slope[:], threshold[:], ALU.mult)
+            negated = sb(name, [P, PACK], F32)
+            nc.gpsimd.tensor_scalar(negated[:], product[:], -1.0, 0.0, ALU.mult, ALU.add)
+            return negated
+
+        bias1 = bias("bias1", sl_t, th_t)
+        bias2 = bias("bias2", sl2_t, th2_t)
+
+        xs_a = sb("xs_a", [P, S], U8)
+        xs_b = sb("xs_b", [P, S], U8)
+        xw_a = sb("xw_a", [P, S], U32)
+        xw_b = sb("xw_b", [P, S], U32)
+        nc.vector.tensor_copy(xs_a[:], xs[:].indirect(offs_t[:]))
+        nc.vector.tensor_copy(xs_b[:], xs[:].indirect(two_t[:]))
+        nc.vector.tensor_copy(xw_a[:], xw[:].indirect(offs_t[:]))
+        nc.vector.tensor_copy(xw_b[:], xw[:].indirect(two_t[:]))
+
+        def product(bank, w, ws, t, words, scales):
+            nc.tensor.matmul_mx(
+                out=bank, lhsT=w[:, t, :].bitcast(FP8X4), lhsT_scale=ws[:, t, :],
+                rhs=words.bitcast(FP8X4), rhs_scale=scales, start=True, stop=True,
+            )
+
+        y_ps = [psum.tile([P, S], F32, name=f"y_ps{t}", tag=f"bank{2 * t}") for t in range(PACK)]
+        d_ps = [psum.tile([P, S], F32, name=f"d_ps{t}", tag=f"bank{2 * t + 1}") for t in range(PACK)]
+        y = [window(f"y{t}", t) for t in range(PACK)]
+        d = [window(f"d{t}", t) for t in range(PACK)]
+
+        for t in range(PACK):
+            product(y_ps[t][:], w1, w1s, t, xw_a[:], xs_a[:])
+        nc.vector.tensor_copy(y[0][:, :S], y_ps[0][:])
+        w2 = deal("w2", w2_raw, U32, 4, nc.vector)
+        for t in range(PACK):
+            product(d_ps[t][:], w2, w2s, t, xw_b[:], xs_b[:])
+        nc.vector.tensor_copy(y[1][:, :S], y_ps[1][:])
+        nc.vector.tensor_copy(d[0][:, :S], d_ps[0][:])
+        nc.vector.tensor_copy(d[1][:, :S], d_ps[1][:])
+        for t in (2, 3):
+            nc.vector.tensor_copy(y[t][:, :S], y_ps[t][:])
+            nc.vector.tensor_copy(d[t][:, :S], d_ps[t][:])
+
+        w3 = deal("w3", w3_raw, U32, 4, nc.gpsimd)
+        w3s = deal("w3s", w3s_raw, U8, 16, nc.gpsimd)
+
+        sg = sb("sg", [P, PACK, S], F32)
+        sg2 = sb("sg2", [P, PACK, S], F32)
+        left = sb("left", [P, PACK, S], F32)
+        right = sb("right", [P, PACK, S], F32)
+        z = sb("z", [P, S, PACK], BF16)
+        z_words = sb("z_words", [P, S], U32)
+        z_scales = sb("z_scales", [P, S], U8)
+        h = [window(f"h{t}", t) for t in range(PACK)]
+        h_ps = [psum.tile([P, S], F32, name=f"h_ps{t}", tag=f"bank{t}") for t in range(PACK)]
+
+        def gate(dst, source, lst, slope, b, t, c):
+            nc.scalar.activation(
+                dst[:, t, c], source[t][:].indirect(offsets(lst, c)), ACT.Sigmoid,
+                bias=b[:, t : t + 1], scale=slope[:, t : t + 1],
+            )
+
+        def term(dst, g, other, t, c):
+            nc.vector.scalar_tensor_tensor(dst[:, t, c], g[:, t, c], gn_t[:, t : t + 1], other[t][:, c], ALU.mult, ALU.mult)
+
+        def interleaved(tile, c):
+            return tile[:, c, :].rearrange("p (a i) t -> p a t i", i=4)
+
+        def planes(tile, c):
+            return tile[:, :, c].rearrange("p t (a i) -> p a t i", i=4)
+
+        def quantise(words, scales, values, c):
+            nc.vector.quantize_mx(out=words[:, c].bitcast(FP8X4), scales=scales[:, c], in_=values[:, c, :].rearrange("p c t -> p (c t)"))
+
+        everything = slice(0, S)
+        for t in (0, 1):
+            gate(sg, y, n1_t, sl_t, bias1, t, everything)
+        for t in (0, 1):
+            gate(sg2, d, n2_t, sl2_t, bias2, t, everything)
+        for t in (0, 1):
+            term(left, sg, d_ps, t, everything)
+        for t in (0, 1):
+            term(right, sg2, y_ps, t, everything)
+        for half in (0, 1):
+            c = cols(half)
+            for t in (2, 3):
+                gate(sg, y, n1_t, sl_t, bias1, t, c)
+                gate(sg2, d, n2_t, sl2_t, bias2, t, c)
+        for t in (2, 3):
+            term(left, sg, d_ps, t, cols(0))
+            term(right, sg2, y_ps, t, cols(0))
+        nc.vector.tensor_tensor(interleaved(z, cols(0)), planes(left, cols(0)), planes(right, cols(0)), ALU.add)
+        term(left, sg, d_ps, 2, cols(1))
+        quantise(z_words, z_scales, z, cols(0))
+        term(right, sg2, y_ps, 2, cols(1))
+        term(left, sg, d_ps, 3, cols(1))
+        term(right, sg2, y_ps, 3, cols(1))
+        nc.vector.tensor_tensor(interleaved(z, cols(1)), planes(left, cols(1)), planes(right, cols(1)), ALU.add)
+        quantise(z_words, z_scales, z, cols(1))
+
+        for t in range(PACK):
+            product(h_ps[t][:, cols(0)], w3, w3s, t, z_words[:, cols(0)], z_scales[:, cols(0)])
+        for t in range(PACK):
+            nc.scalar.copy(h[t][:, cols(0)], h_ps[t][:, cols(0)])
+        for t in range(PACK):
+            product(h_ps[t][:, cols(1)], w3, w3s, t, z_words[:, cols(1)], z_scales[:, cols(1)])
+        nc.scalar.copy(h[0][:, cols(1)], h_ps[0][:, cols(1)])
+        for t in range(1, PACK):
+            nc.vector.tensor_copy(h[t][:, cols(1)], h_ps[t][:, cols(1)])
+
+        h3 = sb("h_at_n3", [P, PACK, S], F32)
+        h4 = sb("h_at_n4", [P, PACK, S], F32)
+        above = sb("above", [P, PACK, S], F32)
+        below = sb("below", [P, PACK, S], F32)
+        hinge = sb("hinge", [P, PACK, S], F32)
+        result = sb("result", [P, PACK, S], F32)
+        rounded = sb("rounded", [P, S, PACK], BF16)
+        o_words = sb("o_words", [P, S], U32)
+        o_scales = sb("o_scales", [P, S], U8)
+        out_rows = out_0.rearrange("(p t) c -> p t c", t=PACK)
+        out_words = out_1[0].rearrange("p n t -> p (n t)").bitcast(I32)
+
+        def fetch(dst, lst, t, c):
+            nc.scalar.activation(dst[:, t, c], h[t][:].indirect(offsets(lst, c)), ACT.Copy)
+
+        pieces = [(0, everything), (1, everything), (2, cols(0)), (3, cols(0)), (2, cols(1)), (3, cols(1))]
+        for t, c in pieces:
+            fetch(h4, n4_t, t, c)
+            fetch(h3, n3_t, t, c)
+
+        def sub_below(t, c):
+            nc.vector.tensor_tensor(below[:, t, c], h4[:, t, c], h[t][:, c], ALU.subtract)
+
+        def half_relu(t, c):
+            nc.vector.tensor_scalar(hinge[:, t, c], below[:, t, c], 0.0, 0.5, ALU.max, ALU.mult)
+
+        def sub_above(t, c):
+            nc.vector.tensor_tensor(above[:, t, c], h[t][:, c], h3[:, t, c], ALU.subtract)
+
+        def finish(t, c):
+            nc.vector.scalar_tensor_tensor(result[:, t, c], above[:, t, c], 0.0, hinge[:, t, c], ALU.max, ALU.add)
+
+        def round_half(c):
+            nc.vector.tensor_copy(interleaved(rounded, c), planes(result, c))
+
+        sub_below(*pieces[0])
+        for i, (t, c) in enumerate(pieces):
+            half_relu(t, c)
+            sub_above(t, c)
+            if i + 1 < len(pieces):
+                sub_below(*pieces[i + 1])
+            if i == 5:
+                quantise(o_words, o_scales, rounded, cols(0))
+                nc.sync.dma_start(out_words[:, cols(0)], o_words[:, cols(0)].bitcast(I32))
+            finish(t, c)
+            if i < 2:
+                nc.sync.dma_start(out_rows[:, t, :], result[:, t, :])
+            if i == 3 or i == 5:
+                nc.sync.dma_start(out_rows[:, 2:4, c], result[:, 2:4, c])
+            if i == 4:
+                round_half(cols(0))
+        round_half(cols(1))
+        quantise(o_words, o_scales, rounded, cols(1))
+        nc.sync.dma_start(out_words[:, cols(1)], o_words[:, cols(1)].bitcast(I32))
+        for q in range(4):
+            queue = nc.scalar if q < 3 else nc.sync
+            queue.dma_start(out_2[0, 4 * q : 4 * q + 4, :].bitcast(I32), o_scales[32 * q : 32 * q + 4, :].bitcast(I32))

@@ -30,36 +30,34 @@ def tile_picked_twlcxbhinge_none_po_kernel(
         keep = ctx.enter_context(tc.tile_pool(name="keep", bufs=1))
         psum = ctx.enter_context(tc.psum_pool(name="psum", bufs=1))
 
-        def sb(name, shape, dtype):
-            return keep.tile(shape, dtype, name=name, align_bytes=64)
+        def sb(name, shape, dtype, tag=None):
+            return keep.tile(shape, dtype, name=name, tag=tag or name, align_bytes=64)
 
         def load_list(name, source):
             tile = keep.tile([P, S // 16], U16, name=name)
             nc.sync.dma_start(tile[:], source)
             return tile
 
-        def load_words(name, source, width):
-            tile = sb(name, [P, width], U32)
+        def load_words(name, source, width, tag=None):
+            tile = sb(name, [P, width], U32, tag)
             nc.sync.dma_start(tile[:].bitcast(I32), source[0].rearrange("p n t -> p (n t)").bitcast(I32))
             return tile
 
-        def zeroed(name, width, engine):
+        def load_scales(name, source, width):
             tile = sb(name, [P, width], U8)
-            engine.memset(tile[:].bitcast(I32), 0)
+            for q in range(4):
+                rows = source[0, 4 * q : 4 * q + 4, :].bitcast(I32)
+                nc.sync.dma_start(tile[32 * q : 32 * q + 32, :].bitcast(I32), rows.partition_broadcast(8))
             return tile
 
-        def load_scale_rows(tile, source, queues):
-            for q in range(4):
-                queues[q].dma_start(tile[32 * q : 32 * q + 4, :].bitcast(I32), source[0, 4 * q : 4 * q + 4, :].bitcast(I32))
-
-        def load_rows(name, source, queue):
-            tile = sb(name, [P, PACK], F32)
+        def load_rows(name, source, queue, tag=None):
+            tile = sb(name, [P, PACK], F32, tag)
             queue.dma_start(tile[:], source.rearrange("(p t) o -> p (t o)", t=PACK))
             return tile
 
-        def deal(name, raw, dtype, run, engine):
-            dealt = sb(name, [P, PACK, P], dtype)
-            engine.tensor_copy(
+        def deal(name, raw, dtype, run, engine, tag=None):
+            dealt = sb(name, [P, PACK, P], dtype, tag)
+            engine(
                 dealt[:].rearrange("p t (a i) -> p a t i", i=run),
                 raw[:].rearrange("p (a i t) -> p a t i", i=run, t=PACK),
             )
@@ -78,53 +76,50 @@ def tile_picked_twlcxbhinge_none_po_kernel(
             nc.vector.memset(tile[:, S:], 0.0)
             return tile
 
-        xs = zeroed("xs", T, nc.vector)
-        w1s_raw = zeroed("w1s_raw", H, nc.gpsimd)
-        w2s_raw = zeroed("w2s_raw", H, nc.vector)
-        w3s_raw = zeroed("w3s_raw", N, nc.vector)
+        y = [window(f"y{t}", t) for t in range(PACK)]
+        d = [window(f"d{t}", t) for t in range(PACK)]
+        warm_in = sb("warm_in", [P, 1], F32)
+        warm_out = sb("warm_out", [P, 1], F32)
+        nc.gpsimd.memset(warm_in[:], 0.0)
+        nc.scalar.activation(warm_out[:], warm_in[:], ACT.Sigmoid)
 
         offs_t = load_list("offs_t", offs)
-        w1_raw = load_words("w1_raw", w1_words, H)
+        w1s_raw = load_scales("w1s_raw", w1_scales, H)
         xw = load_words("xw", x_words, T)
-        load_scale_rows(w1s_raw, w1_scales, [nc.gpsimd, nc.gpsimd, nc.gpsimd, nc.scalar])
-        load_scale_rows(xs, x_scales, [nc.scalar] * 4)
         two_t = load_list("two_t", two)
+        w1_raw = load_words("w1_raw", w1_words, H)
+        xs = load_scales("xs", x_scales, T)
         w2_raw = load_words("w2_raw", w2_words, H)
-        load_scale_rows(w2s_raw, w2_scales, [nc.scalar] * 4)
         n1_t = load_list("n1_t", n1)
-        sl_t = load_rows("sl_t", sl, nc.sync)
-        th_t = load_rows("th_t", th, nc.sync)
+        w2s_raw = load_scales("w2s_raw", w2_scales, H)
         n2_t = load_list("n2_t", n2)
+        sl_t = load_rows("sl_t", sl, nc.gpsimd)
+        th_t = load_rows("th_t", th, nc.gpsimd)
         sl2_t = load_rows("sl2_t", sl2, nc.sync)
         th2_t = load_rows("th2_t", th2, nc.sync)
-        gn_t = load_rows("gn_t", gn, nc.sync)
+        gn_t = load_rows("gn_t", gn, nc.gpsimd)
         w3_raw = load_words("w3_raw", w3_words, N)
-        load_scale_rows(w3s_raw, w3_scales, [nc.sync] * 4)
-        n3_t = load_list("n3_t", n3)
+        w3s_raw = load_scales("w3s_raw", w3_scales, N)
         n4_t = load_list("n4_t", n4)
+        n3_t = load_list("n3_t", n3)
 
-        w1 = deal("w1", w1_raw, U32, 4, nc.vector)
-        w1s = deal("w1s", w1s_raw, U8, 16, nc.vector)
-        w2s = deal("w2s", w2s_raw, U8, 16, nc.vector)
-
-        def bias(name, slope, threshold):
-            product = sb(name + "_product", [P, PACK], F32)
-            nc.gpsimd.tensor_tensor(product[:], slope[:], threshold[:], ALU.mult)
-            negated = sb(name, [P, PACK], F32)
-            nc.gpsimd.tensor_scalar(negated[:], product[:], -1.0, 0.0, ALU.mult, ALU.add)
+        def bias(name, slope, threshold, tag=None):
+            negated = sb(name, [P, PACK], F32, tag)
+            nc.vector.scalar_tensor_tensor(negated[:], slope[:], -1.0, threshold[:], ALU.mult, ALU.mult)
             return negated
-
-        bias1 = bias("bias1", sl_t, th_t)
-        bias2 = bias("bias2", sl2_t, th2_t)
 
         xs_a = sb("xs_a", [P, S], U8)
         xs_b = sb("xs_b", [P, S], U8)
         xw_a = sb("xw_a", [P, S], U32)
         xw_b = sb("xw_b", [P, S], U32)
-        nc.vector.tensor_copy(xs_a[:], xs[:].indirect(offs_t[:]))
-        nc.vector.tensor_copy(xs_b[:], xs[:].indirect(two_t[:]))
+        w1s = deal("w1s", w1s_raw, U8, 16, nc.vector.tensor_copy)
+        w1 = deal("w1", w1_raw, U32, 4, nc.scalar.copy)
+        w2 = deal("w2", w2_raw, U32, 4, nc.scalar.copy)
         nc.vector.tensor_copy(xw_a[:], xw[:].indirect(offs_t[:]))
         nc.vector.tensor_copy(xw_b[:], xw[:].indirect(two_t[:]))
+        nc.vector.tensor_copy(xs_a[:], xs[:].indirect(offs_t[:]))
+        nc.vector.tensor_copy(xs_b[:], xs[:].indirect(two_t[:]))
+        bias1 = bias("bias1", sl_t, th_t, "w1_raw")
 
         def product(bank, w, ws, t, words, scales):
             nc.tensor.matmul_mx(
@@ -134,24 +129,23 @@ def tile_picked_twlcxbhinge_none_po_kernel(
 
         y_ps = [psum.tile([P, S], F32, name=f"y_ps{t}", tag=f"bank{2 * t}") for t in range(PACK)]
         d_ps = [psum.tile([P, S], F32, name=f"d_ps{t}", tag=f"bank{2 * t + 1}") for t in range(PACK)]
-        y = [window(f"y{t}", t) for t in range(PACK)]
-        d = [window(f"d{t}", t) for t in range(PACK)]
 
         for t in range(PACK):
             product(y_ps[t][:], w1, w1s, t, xw_a[:], xs_a[:])
-        nc.vector.tensor_copy(y[0][:, :S], y_ps[0][:])
-        w2 = deal("w2", w2_raw, U32, 4, nc.vector)
-        for t in range(PACK):
-            product(d_ps[t][:], w2, w2s, t, xw_b[:], xs_b[:])
+        nc.scalar.copy(y[0][:, :S], y_ps[0][:])
         nc.vector.tensor_copy(y[1][:, :S], y_ps[1][:])
-        nc.vector.tensor_copy(d[0][:, :S], d_ps[0][:])
-        nc.vector.tensor_copy(d[1][:, :S], d_ps[1][:])
+        w2s = deal("w2s", w2s_raw, U8, 16, nc.vector.tensor_copy)
         for t in (2, 3):
             nc.vector.tensor_copy(y[t][:, :S], y_ps[t][:])
+        for t in range(PACK):
+            product(d_ps[t][:], w2, w2s, t, xw_b[:], xs_b[:])
+        bias2 = bias("bias2", sl2_t, th2_t, "w2s_raw")
+        nc.scalar.copy(d[0][:, :S], d_ps[0][:])
+        for t in range(1, PACK):
             nc.vector.tensor_copy(d[t][:, :S], d_ps[t][:])
 
-        w3 = deal("w3", w3_raw, U32, 4, nc.gpsimd)
-        w3s = deal("w3s", w3s_raw, U8, 16, nc.gpsimd)
+        w3 = deal("w3", w3_raw, U32, 4, nc.gpsimd.tensor_copy)
+        w3s = deal("w3s", w3s_raw, U8, 16, nc.gpsimd.tensor_copy)
 
         sg = sb("sg", [P, PACK, S], F32)
         sg2 = sb("sg2", [P, PACK, S], F32)
@@ -182,22 +176,18 @@ def tile_picked_twlcxbhinge_none_po_kernel(
             nc.vector.quantize_mx(out=words[:, c].bitcast(FP8X4), scales=scales[:, c], in_=values[:, c, :].rearrange("p c t -> p (c t)"))
 
         everything = slice(0, S)
-        for t in (0, 1):
-            gate(sg, y, n1_t, sl_t, bias1, t, everything)
-        for t in (0, 1):
-            gate(sg2, d, n2_t, sl2_t, bias2, t, everything)
-        for t in (0, 1):
-            term(left, sg, d_ps, t, everything)
-        for t in (0, 1):
-            term(right, sg2, y_ps, t, everything)
-        for half in (0, 1):
-            c = cols(half)
-            for t in (2, 3):
-                gate(sg, y, n1_t, sl_t, bias1, t, c)
-                gate(sg2, d, n2_t, sl2_t, bias2, t, c)
+        first = [(0, everything), (1, everything), (2, cols(0)), (3, cols(0))]
+        for t, c in first:
+            gate(sg, y, n1_t, sl_t, bias1, t, c)
+        for t, c in first:
+            gate(sg2, d, n2_t, sl2_t, bias2, t, c)
         for t in (2, 3):
-            term(left, sg, d_ps, t, cols(0))
-            term(right, sg2, y_ps, t, cols(0))
+            gate(sg, y, n1_t, sl_t, bias1, t, cols(1))
+            gate(sg2, d, n2_t, sl2_t, bias2, t, cols(1))
+        for t, c in first:
+            term(left, sg, d_ps, t, c)
+        for t, c in first:
+            term(right, sg2, y_ps, t, c)
         nc.vector.tensor_tensor(interleaved(z, cols(0)), planes(left, cols(0)), planes(right, cols(0)), ALU.add)
         term(left, sg, d_ps, 2, cols(1))
         quantise(z_words, z_scales, z, cols(0))

@@ -18,7 +18,6 @@ ACT = mybir.ActivationFunctionType
 P = 128
 PACK = 4
 HALF = S // 2
-WHOLE = (0, 1)
 
 
 def tile_picked_twlcxbhinge_none_po_kernel(
@@ -43,24 +42,27 @@ def tile_picked_twlcxbhinge_none_po_kernel(
             nc.sync.dma_start(tile[:].bitcast(I32), source[0].rearrange("p n t -> p (n t)").bitcast(I32))
             return tile
 
-        def load_scales(name, source, width):
+        def zeroed(name, width):
             tile = sb(name, [P, width], U8)
-            for q in range(4):
-                rows = source[0, 4 * q : 4 * q + 4, :].bitcast(I32)
-                nc.sync.dma_start(tile[32 * q : 32 * q + 32, :].bitcast(I32), rows.partition_broadcast(8))
+            nc.vector.memset(tile[:].bitcast(I32), 0)
             return tile
+
+        def load_scales(tile, source):
+            for q in range(4):
+                nc.sync.dma_start(tile[32 * q : 32 * q + 4, :].bitcast(I32), source[0, 4 * q : 4 * q + 4, :].bitcast(I32))
 
         def load_rows(name, source, queue, tag=None):
             tile = sb(name, [P, PACK], F32, tag)
             queue.dma_start(tile[:], source.rearrange("(p t) o -> p (t o)", t=PACK))
             return tile
 
-        def deal(name, raw, dtype, run, engine, tag=None):
-            dealt = sb(name, [P, PACK, P], dtype, tag)
-            engine(
-                dealt[:].rearrange("p t (a i) -> p a t i", i=run),
-                raw[:].rearrange("p (a i t) -> p a t i", i=run, t=PACK),
-            )
+        def deal(name, raw, dtype, run, copy, parts=1):
+            dealt = sb(name, [P, PACK, P], dtype)
+            dst = dealt[:].rearrange("p t (a i) -> p a t i", i=run)
+            src = raw[:].rearrange("p (a i t) -> p a t i", i=run, t=PACK)
+            step = PACK // parts
+            for t in range(0, PACK, step):
+                copy(dst[:, :, t : t + step, :], src[:, :, t : t + step, :])
             return dealt
 
         def cols(half):
@@ -69,57 +71,61 @@ def tile_picked_twlcxbhinge_none_po_kernel(
         def offsets(lst, c):
             return lst[:, c.start // 16 : c.stop // 16]
 
-        def window(name, t):
-            if t not in WHOLE:
-                return sb(name, [P, S], F32)
+        def window(name):
             tile = sb(name, [P, 2 * S], F32)
             nc.vector.memset(tile[:, S:], 0.0)
             return tile
 
-        y = [window(f"y{t}", t) for t in range(PACK)]
-        d = [window(f"d{t}", t) for t in range(PACK)]
+        xs = zeroed("xs", T)
+        w1s_raw = zeroed("w1s_raw", H)
+        w2s_raw = zeroed("w2s_raw", H)
+        w3s_raw = zeroed("w3s_raw", N)
+        y = [window(f"y{t}") for t in range(PACK)]
+        d = [sb(f"d{t}", [P, S], F32) for t in range(PACK)]
         warm_in = sb("warm_in", [P, 1], F32)
         warm_out = sb("warm_out", [P, 1], F32)
         nc.gpsimd.memset(warm_in[:], 0.0)
         nc.scalar.activation(warm_out[:], warm_in[:], ACT.Sigmoid)
 
         offs_t = load_list("offs_t", offs)
-        w1s_raw = load_scales("w1s_raw", w1_scales, H)
-        xw = load_words("xw", x_words, T)
-        two_t = load_list("two_t", two)
         w1_raw = load_words("w1_raw", w1_words, H)
-        xs = load_scales("xs", x_scales, T)
+        load_scales(xs, x_scales)
+        two_t = load_list("two_t", two)
+        xw = load_words("xw", x_words, T)
+        load_scales(w1s_raw, w1_scales)
         w2_raw = load_words("w2_raw", w2_words, H)
         n1_t = load_list("n1_t", n1)
-        w2s_raw = load_scales("w2s_raw", w2_scales, H)
+        load_scales(w2s_raw, w2_scales)
         n2_t = load_list("n2_t", n2)
         sl_t = load_rows("sl_t", sl, nc.gpsimd)
         th_t = load_rows("th_t", th, nc.gpsimd)
         sl2_t = load_rows("sl2_t", sl2, nc.sync)
         th2_t = load_rows("th2_t", th2, nc.sync)
-        gn_t = load_rows("gn_t", gn, nc.gpsimd)
+        gn_t = load_rows("gn_t", gn, nc.sync)
         w3_raw = load_words("w3_raw", w3_words, N)
-        w3s_raw = load_scales("w3s_raw", w3_scales, N)
+        load_scales(w3s_raw, w3_scales)
         n4_t = load_list("n4_t", n4)
         n3_t = load_list("n3_t", n3)
 
-        def bias(name, slope, threshold, tag=None):
-            negated = sb(name, [P, PACK], F32, tag)
-            nc.vector.scalar_tensor_tensor(negated[:], slope[:], -1.0, threshold[:], ALU.mult, ALU.mult)
+        def bias(name, slope, threshold):
+            product = sb(name + "_product", [P, PACK], F32)
+            nc.gpsimd.tensor_tensor(product[:], slope[:], threshold[:], ALU.mult)
+            negated = sb(name, [P, PACK], F32)
+            nc.gpsimd.tensor_scalar(negated[:], product[:], -1.0, 0.0, ALU.mult, ALU.add)
             return negated
 
         xs_a = sb("xs_a", [P, S], U8)
         xs_b = sb("xs_b", [P, S], U8)
         xw_a = sb("xw_a", [P, S], U32)
-        xw_b = sb("xw_b", [P, S], U32)
-        w1s = deal("w1s", w1s_raw, U8, 16, nc.vector.tensor_copy)
         w1 = deal("w1", w1_raw, U32, 4, nc.scalar.copy)
-        w2 = deal("w2", w2_raw, U32, 4, nc.scalar.copy)
-        nc.vector.tensor_copy(xw_a[:], xw[:].indirect(offs_t[:]))
-        nc.vector.tensor_copy(xw_b[:], xw[:].indirect(two_t[:]))
         nc.vector.tensor_copy(xs_a[:], xs[:].indirect(offs_t[:]))
         nc.vector.tensor_copy(xs_b[:], xs[:].indirect(two_t[:]))
-        bias1 = bias("bias1", sl_t, th_t, "w1_raw")
+        nc.vector.tensor_copy(xw_a[:], xw[:].indirect(offs_t[:]))
+        w1s = deal("w1s", w1s_raw, U8, 16, nc.vector.tensor_copy)
+        xw_b = sb("xw_b", [P, S], U32, "w1s_raw")
+        nc.vector.tensor_copy(xw_b[:], xw[:].indirect(two_t[:]))
+        bias1 = bias("bias1", sl_t, th_t)
+        w2 = deal("w2", w2_raw, U32, 4, nc.scalar.copy)
 
         def product(bank, w, ws, t, words, scales):
             nc.tensor.matmul_mx(
@@ -132,17 +138,14 @@ def tile_picked_twlcxbhinge_none_po_kernel(
 
         for t in range(PACK):
             product(y_ps[t][:], w1, w1s, t, xw_a[:], xs_a[:])
-        nc.scalar.copy(y[0][:, :S], y_ps[0][:])
-        nc.vector.tensor_copy(y[1][:, :S], y_ps[1][:])
-        w2s = deal("w2s", w2s_raw, U8, 16, nc.vector.tensor_copy)
-        for t in (2, 3):
+        for t in range(PACK):
             nc.vector.tensor_copy(y[t][:, :S], y_ps[t][:])
+        w2s = deal("w2s", w2s_raw, U8, 16, nc.gpsimd.tensor_copy)
         for t in range(PACK):
             product(d_ps[t][:], w2, w2s, t, xw_b[:], xs_b[:])
-        bias2 = bias("bias2", sl2_t, th2_t, "w2s_raw")
-        nc.scalar.copy(d[0][:, :S], d_ps[0][:])
-        for t in range(1, PACK):
-            nc.vector.tensor_copy(d[t][:, :S], d_ps[t][:])
+        bias2 = bias("bias2", sl2_t, th2_t)
+        for t in range(PACK):
+            nc.vector.tensor_copy(d[t][:], d_ps[t][:])
 
         w3 = deal("w3", w3_raw, U32, 4, nc.gpsimd.tensor_copy)
         w3s = deal("w3s", w3s_raw, U8, 16, nc.gpsimd.tensor_copy)
@@ -154,8 +157,8 @@ def tile_picked_twlcxbhinge_none_po_kernel(
         z = sb("z", [P, S, PACK], BF16)
         z_words = sb("z_words", [P, S], U32)
         z_scales = sb("z_scales", [P, S], U8)
-        h = [window(f"h{t}", t) for t in range(PACK)]
-        h_ps = [psum.tile([P, S], F32, name=f"h_ps{t}", tag=f"bank{t}") for t in range(PACK)]
+        h = [window(f"h{t}") for t in range(PACK)]
+        h_ps = [[psum.tile([P, HALF], F32, name=f"h_ps{half}{t}", tag=f"bank{PACK * half + t}") for t in range(PACK)] for half in (0, 1)]
 
         def gate(dst, source, lst, slope, b, t, c):
             nc.scalar.activation(
@@ -176,36 +179,32 @@ def tile_picked_twlcxbhinge_none_po_kernel(
             nc.vector.quantize_mx(out=words[:, c].bitcast(FP8X4), scales=scales[:, c], in_=values[:, c, :].rearrange("p c t -> p (c t)"))
 
         everything = slice(0, S)
-        first = [(0, everything), (1, everything), (2, cols(0)), (3, cols(0))]
-        for t, c in first:
-            gate(sg, y, n1_t, sl_t, bias1, t, c)
-        for t, c in first:
-            gate(sg2, d, n2_t, sl2_t, bias2, t, c)
-        for t in (2, 3):
-            gate(sg, y, n1_t, sl_t, bias1, t, cols(1))
-            gate(sg2, d, n2_t, sl2_t, bias2, t, cols(1))
-        for t, c in first:
-            term(left, sg, d_ps, t, c)
-        for t, c in first:
-            term(right, sg2, y_ps, t, c)
+        for t in range(PACK):
+            gate(sg, y, n1_t, sl_t, bias1, t, everything)
+        for t in range(PACK):
+            term(left, sg, d_ps, t, everything)
+        for half in (0, 1):
+            for t in range(PACK):
+                gate(sg2, d, n2_t, sl2_t, bias2, t, cols(half))
+        for t in range(PACK):
+            term(right, sg2, y_ps, t, cols(0))
         nc.vector.tensor_tensor(interleaved(z, cols(0)), planes(left, cols(0)), planes(right, cols(0)), ALU.add)
-        term(left, sg, d_ps, 2, cols(1))
+        term(right, sg2, y_ps, 0, cols(1))
         quantise(z_words, z_scales, z, cols(0))
-        term(right, sg2, y_ps, 2, cols(1))
-        term(left, sg, d_ps, 3, cols(1))
-        term(right, sg2, y_ps, 3, cols(1))
+        for t in range(1, PACK):
+            term(right, sg2, y_ps, t, cols(1))
         nc.vector.tensor_tensor(interleaved(z, cols(1)), planes(left, cols(1)), planes(right, cols(1)), ALU.add)
         quantise(z_words, z_scales, z, cols(1))
 
         for t in range(PACK):
-            product(h_ps[t][:, cols(0)], w3, w3s, t, z_words[:, cols(0)], z_scales[:, cols(0)])
+            product(h_ps[0][t][:], w3, w3s, t, z_words[:, cols(0)], z_scales[:, cols(0)])
         for t in range(PACK):
-            nc.scalar.copy(h[t][:, cols(0)], h_ps[t][:, cols(0)])
+            nc.scalar.copy(h[t][:, cols(0)], h_ps[0][t][:])
         for t in range(PACK):
-            product(h_ps[t][:, cols(1)], w3, w3s, t, z_words[:, cols(1)], z_scales[:, cols(1)])
-        nc.scalar.copy(h[0][:, cols(1)], h_ps[0][:, cols(1)])
-        for t in range(1, PACK):
-            nc.vector.tensor_copy(h[t][:, cols(1)], h_ps[t][:, cols(1)])
+            product(h_ps[1][t][:], w3, w3s, t, z_words[:, cols(1)], z_scales[:, cols(1)])
+        for t in range(PACK):
+            copy = nc.scalar.copy if t == 1 else nc.vector.tensor_copy
+            copy(h[t][:, cols(1)], h_ps[1][t][:])
 
         h3 = sb("h_at_n3", [P, PACK, S], F32)
         h4 = sb("h_at_n4", [P, PACK, S], F32)
@@ -222,10 +221,11 @@ def tile_picked_twlcxbhinge_none_po_kernel(
         def fetch(dst, lst, t, c):
             nc.scalar.activation(dst[:, t, c], h[t][:].indirect(offsets(lst, c)), ACT.Copy)
 
-        pieces = [(0, everything), (1, everything), (2, cols(0)), (3, cols(0)), (2, cols(1)), (3, cols(1))]
-        for t, c in pieces:
-            fetch(h4, n4_t, t, c)
-            fetch(h3, n3_t, t, c)
+        for t in range(PACK):
+            fetch(h4, n4_t, t, everything)
+        for half in (0, 1):
+            for t in range(PACK):
+                fetch(h3, n3_t, t, cols(half))
 
         def sub_below(t, c):
             nc.vector.tensor_tensor(below[:, t, c], h4[:, t, c], h[t][:, c], ALU.subtract)
@@ -237,28 +237,31 @@ def tile_picked_twlcxbhinge_none_po_kernel(
             nc.vector.tensor_tensor(above[:, t, c], h[t][:, c], h3[:, t, c], ALU.subtract)
 
         def finish(t, c):
-            nc.vector.scalar_tensor_tensor(result[:, t, c], above[:, t, c], 0.0, hinge[:, t, c], ALU.max, ALU.add)
+            pair = slice(t, t + 2)
+            nc.vector.scalar_tensor_tensor(result[:, pair, c], above[:, pair, c], 0.0, hinge[:, pair, c], ALU.max, ALU.add)
 
-        def round_half(c):
-            nc.vector.tensor_copy(interleaved(rounded, c), planes(result, c))
+        def round_half(c, copy):
+            copy(interleaved(rounded, c), planes(result, c))
 
-        sub_below(*pieces[0])
-        for i, (t, c) in enumerate(pieces):
-            half_relu(t, c)
-            sub_above(t, c)
-            if i + 1 < len(pieces):
-                sub_below(*pieces[i + 1])
-            if i == 5:
-                quantise(o_words, o_scales, rounded, cols(0))
-                nc.sync.dma_start(out_words[:, cols(0)], o_words[:, cols(0)].bitcast(I32))
-            finish(t, c)
-            if i < 2:
-                nc.sync.dma_start(out_rows[:, t, :], result[:, t, :])
-            if i == 3 or i == 5:
-                nc.sync.dma_start(out_rows[:, 2:4, c], result[:, 2:4, c])
-            if i == 4:
-                round_half(cols(0))
-        round_half(cols(1))
+        for t in range(PACK):
+            sub_below(t, everything)
+            half_relu(t, everything)
+        for t in range(PACK):
+            sub_above(t, cols(0))
+        finish(0, cols(0))
+        finish(2, cols(0))
+        nc.sync.dma_start(out_rows[:, :, cols(0)], result[:, :, cols(0)])
+        sub_above(0, cols(1))
+        sub_above(1, cols(1))
+        round_half(cols(0), nc.scalar.copy)
+        finish(0, cols(1))
+        sub_above(2, cols(1))
+        sub_above(3, cols(1))
+        quantise(o_words, o_scales, rounded, cols(0))
+        nc.sync.dma_start(out_words[:, cols(0)], o_words[:, cols(0)].bitcast(I32))
+        finish(2, cols(1))
+        nc.sync.dma_start(out_rows[:, :, cols(1)], result[:, :, cols(1)])
+        round_half(cols(1), nc.vector.tensor_copy)
         quantise(o_words, o_scales, rounded, cols(1))
         nc.sync.dma_start(out_words[:, cols(1)], o_words[:, cols(1)].bitcast(I32))
         for q in range(4):

from contextlib import ExitStack

import concourse.mybir as mybir

K, T, S, N, H = 512, 2048, 256, 512, 512
FLOPS = 2 * K * H * S * 2 + 2 * H * N * S

F32 = mybir.dt.float32
BF16 = mybir.dt.bfloat16
I32 = mybir.dt.int32
U32 = mybir.dt.uint32
U16 = mybir.dt.uint16
U8 = mybir.dt.uint8
FP8X4 = mybir.dt.float8_e4m3fn_x4
ALU = mybir.AluOpType
ACT = mybir.ActivationFunctionType

P = 128
PACK = 4
HALF = S // 2


def tile_picked_twlcxbhinge_none_po_kernel(
    tc, x_words, x_scales, w1_words, w1_scales, w2_words, w2_scales, sl, th, sl2, th2, gn, w3_words, w3_scales,
    offs, two, n1, n2, n3, n4, out_0, out_1, out_2,
):
    nc = tc.nc
    with ExitStack() as ctx:
        keep = ctx.enter_context(tc.tile_pool(name="keep", bufs=1))
        psum = ctx.enter_context(tc.psum_pool(name="psum", bufs=1))

        def sb(name, shape, dtype, tag=None):
            return keep.tile(shape, dtype, name=name, tag=tag or name, align_bytes=64)

        def load_list(name, source):
            tile = keep.tile([P, S // 16], U16, name=name)
            nc.sync.dma_start(tile[:], source)
            return tile

        def load_words(name, source, width, tag=None):
            tile = sb(name, [P, width], U32, tag)
            nc.sync.dma_start(tile[:].bitcast(I32), source[0].rearrange("p n t -> p (n t)").bitcast(I32))
            return tile

        def zeroed(name, width):
            tile = sb(name, [P, width], U8)
            nc.vector.memset(tile[:].bitcast(I32), 0)
            return tile

        def load_scales(tile, source):
            for q in range(4):
                nc.sync.dma_start(tile[32 * q : 32 * q + 4, :].bitcast(I32), source[0, 4 * q : 4 * q + 4, :].bitcast(I32))

        def load_rows(name, source, queue, tag=None):
            tile = sb(name, [P, PACK], F32, tag)
            queue.dma_start(tile[:], source.rearrange("(p t) o -> p (t o)", t=PACK))
            return tile

        def deal(name, raw, dtype, run, copy, parts=1):
            dealt = sb(name, [P, PACK, P], dtype)
            dst = dealt[:].rearrange("p t (a i) -> p a t i", i=run)
            src = raw[:].rearrange("p (a i t) -> p a t i", i=run, t=PACK)
            step = PACK // parts
            for t in range(0, PACK, step):
                copy(dst[:, :, t : t + step, :], src[:, :, t : t + step, :])
            return dealt

        def cols(half):
            return slice(half * HALF, (half + 1) * HALF)

        def offsets(lst, c):
            return lst[:, c.start // 16 : c.stop // 16]

        def window(name):
            tile = sb(name, [P, 2 * S], F32)
            nc.vector.memset(tile[:, S:], 0.0)
            return tile

        xs = zeroed("xs", T)
        w1s_raw = zeroed("w1s_raw", H)
        w2s_raw = zeroed("w2s_raw", H)
        w3s_raw = zeroed("w3s_raw", N)
        y = [window(f"y{t}") for t in range(PACK)]
        d = [sb(f"d{t}", [P, S], F32) for t in range(PACK)]
        warm_in = sb("warm_in", [P, 1], F32)
        warm_out = sb("warm_out", [P, 1], F32)
        nc.gpsimd.memset(warm_in[:], 0.0)
        nc.scalar.activation(warm_out[:], warm_in[:], ACT.Sigmoid)

        offs_t = load_list("offs_t", offs)
        w1_raw = load_words("w1_raw", w1_words, H)
        load_scales(xs, x_scales)
        two_t = load_list("two_t", two)
        xw = load_words("xw", x_words, T)
        load_scales(w1s_raw, w1_scales)
        w2_raw = load_words("w2_raw", w2_words, H)
        n1_t = load_list("n1_t", n1)
        load_scales(w2s_raw, w2_scales)
        n2_t = load_list("n2_t", n2)
        sl_t = load_rows("sl_t", sl, nc.gpsimd)
        th_t = load_rows("th_t", th, nc.gpsimd)
        sl2_t = load_rows("sl2_t", sl2, nc.sync)
        th2_t = load_rows("th2_t", th2, nc.sync)
        gn_t = load_rows("gn_t", gn, nc.sync)
        w3_raw = load_words("w3_raw", w3_words, N)
        load_scales(w3s_raw, w3_scales)
        n4_t = load_list("n4_t", n4)
        n3_t = load_list("n3_t", n3)

        def bias(name, slope, threshold):
            product = sb(name + "_product", [P, PACK], F32)
            nc.gpsimd.tensor_tensor(product[:], slope[:], threshold[:], ALU.mult)
            negated = sb(name, [P, PACK], F32)
            nc.gpsimd.tensor_scalar(negated[:], product[:], -1.0, 0.0, ALU.mult, ALU.add)
            return negated

        xs_a = sb("xs_a", [P, S], U8)
        xs_b = sb("xs_b", [P, S], U8)
        xw_a = sb("xw_a", [P, S], U32)
        w1 = deal("w1", w1_raw, U32, 4, nc.scalar.copy)
        nc.vector.tensor_copy(xs_a[:], xs[:].indirect(offs_t[:]))
        nc.vector.tensor_copy(xs_b[:], xs[:].indirect(two_t[:]))
        nc.vector.tensor_copy(xw_a[:], xw[:].indirect(offs_t[:]))
        w1s = deal("w1s", w1s_raw, U8, 16, nc.vector.tensor_copy)
        xw_b = sb("xw_b", [P, S], U32, "w1s_raw")
        nc.vector.tensor_copy(xw_b[:], xw[:].indirect(two_t[:]))
        bias1 = bias("bias1", sl_t, th_t)
        w2 = deal("w2", w2_raw, U32, 4, nc.scalar.copy)

        def product(bank, w, ws, t, words, scales):
            nc.tensor.matmul_mx(
                out=bank, lhsT=w[:, t, :].bitcast(FP8X4), lhsT_scale=ws[:, t, :],
                rhs=words.bitcast(FP8X4), rhs_scale=scales, start=True, stop=True,
            )

        y_ps = [psum.tile([P, S], F32, name=f"y_ps{t}", tag=f"bank{2 * t}") for t in range(PACK)]
        d_ps = [psum.tile([P, S], F32, name=f"d_ps{t}", tag=f"bank{2 * t + 1}") for t in range(PACK)]

        for t in range(PACK):
            product(y_ps[t][:], w1, w1s, t, xw_a[:], xs_a[:])
        for t in range(PACK):
            nc.vector.tensor_copy(y[t][:, :S], y_ps[t][:])
        w2s = deal("w2s", w2s_raw, U8, 16, nc.gpsimd.tensor_copy)
        for t in range(PACK):
            product(d_ps[t][:], w2, w2s, t, xw_b[:], xs_b[:])
        bias2 = bias("bias2", sl2_t, th2_t)
        for t in range(PACK):
            nc.vector.tensor_copy(d[t][:], d_ps[t][:])

        w3 = deal("w3", w3_raw, U32, 4, nc.gpsimd.tensor_copy)
        w3s = deal("w3s", w3s_raw, U8, 16, nc.gpsimd.tensor_copy)

        sg = sb("sg", [P, PACK, S], F32)
        sg2 = sb("sg2", [P, PACK, S], F32)
        left = sb("left", [P, PACK, S], F32)
        right = sb("right", [P, PACK, S], F32)
        z = sb("z", [P, S, PACK], BF16)
        z_words = sb("z_words", [P, S], U32)
        z_scales = sb("z_scales", [P, S], U8)
        h = [window(f"h{t}") for t in range(PACK)]
        h_ps = [[psum.tile([P, HALF], F32, name=f"h_ps{half}{t}", tag=f"bank{PACK * half + t}") for t in range(PACK)] for half in (0, 1)]

        def gate(dst, source, lst, slope, b, t, c):
            nc.scalar.activation(
                dst[:, t, c], source[t][:].indirect(offsets(lst, c)), ACT.Sigmoid,
                bias=b[:, t : t + 1], scale=slope[:, t : t + 1],
            )

        def term(dst, g, other, t, c):
            nc.vector.scalar_tensor_tensor(dst[:, t, c], g[:, t, c], gn_t[:, t : t + 1], other[t][:, c], ALU.mult, ALU.mult)

        def interleaved(tile, c):
            return tile[:, c, :].rearrange("p (a i) t -> p a t i", i=4)

        def planes(tile, c):
            return tile[:, :, c].rearrange("p t (a i) -> p a t i", i=4)

        def quantise(words, scales, values, c):
            nc.vector.quantize_mx(out=words[:, c].bitcast(FP8X4), scales=scales[:, c], in_=values[:, c, :].rearrange("p c t -> p (c t)"))

        everything = slice(0, S)
        for t in range(PACK):
            gate(sg, y, n1_t, sl_t, bias1, t, everything)
        for t in range(PACK):
            term(left, sg, d_ps, t, everything)
        for half in (0, 1):
            for t in range(PACK):
                gate(sg2, d, n2_t, sl2_t, bias2, t, cols(half))
        for t in range(PACK):
            term(right, sg2, y_ps, t, cols(0))
        nc.vector.tensor_tensor(interleaved(z, cols(0)), planes(left, cols(0)), planes(right, cols(0)), ALU.add)
        term(right, sg2, y_ps, 0, cols(1))
        quantise(z_words, z_scales, z, cols(0))
        for t in range(1, PACK):
            term(right, sg2, y_ps, t, cols(1))
        nc.vector.tensor_tensor(interleaved(z, cols(1)), planes(left, cols(1)), planes(right, cols(1)), ALU.add)
        quantise(z_words, z_scales, z, cols(1))

        for t in range(PACK):
            product(h_ps[0][t][:], w3, w3s, t, z_words[:, cols(0)], z_scales[:, cols(0)])
        for t in range(PACK):
            nc.scalar.copy(h[t][:, cols(0)], h_ps[0][t][:])
        for t in range(PACK):
            product(h_ps[1][t][:], w3, w3s, t, z_words[:, cols(1)], z_scales[:, cols(1)])
        for t in range(PACK):
            copy = nc.scalar.copy if t == 1 else nc.vector.tensor_copy
            copy(h[t][:, cols(1)], h_ps[1][t][:])

        h3 = sb("h_at_n3", [P, PACK, S], F32)
        h4 = sb("h_at_n4", [P, PACK, S], F32)
        above = sb("above", [P, PACK, S], F32)
        below = sb("below", [P, PACK, S], F32)
        hinge = sb("hinge", [P, PACK, S], F32)
        result = sb("result", [P, PACK, S], F32)
        rounded = sb("rounded", [P, S, PACK], BF16)
        o_words = sb("o_words", [P, S], U32)
        o_scales = sb("o_scales", [P, S], U8)
        out_rows = out_0.rearrange("(p t) c -> p t c", t=PACK)
        out_words = out_1[0].rearrange("p n t -> p (n t)").bitcast(I32)

        def fetch(dst, lst, t, c):
            nc.scalar.activation(dst[:, t, c], h[t][:].indirect(offsets(lst, c)), ACT.Copy)

        for t in range(PACK):
            fetch(h4, n4_t, t, everything)
        for half in (0, 1):
            for t in range(PACK):
                fetch(h3, n3_t, t, cols(half))

        def sub_below(t, c):
            nc.vector.tensor_tensor(below[:, t, c], h4[:, t, c], h[t][:, c], ALU.subtract)

        def half_relu(t, c):
            nc.vector.tensor_scalar(hinge[:, t, c], below[:, t, c], 0.0, 0.5, ALU.max, ALU.mult)

        def sub_above(t, c):
            nc.vector.tensor_tensor(above[:, t, c], h[t][:, c], h3[:, t, c], ALU.subtract)

        def finish(t, c):
            pair = slice(t, t + 2)
            nc.vector.scalar_tensor_tensor(result[:, pair, c], above[:, pair, c], 0.0, hinge[:, pair, c], ALU.max, ALU.add)

        def round_half(c, copy):
            copy(interleaved(rounded, c), planes(result, c))

        for t in range(PACK):
            sub_below(t, everything)
            half_relu(t, everything)
        for t in range(PACK):
            sub_above(t, cols(0))
        finish(0, cols(0))
        finish(2, cols(0))
        nc.sync.dma_start(out_rows[:, :, cols(0)], result[:, :, cols(0)])
        sub_above(0, cols(1))
        sub_above(1, cols(1))
        round_half(cols(0), nc.scalar.copy)
        finish(0, cols(1))
        sub_above(2, cols(1))
        sub_above(3, cols(1))
        quantise(o_words, o_scales, rounded, cols(0))
        nc.sync.dma_start(out_words[:, cols(0)], o_words[:, cols(0)].bitcast(I32))
        finish(2, cols(1))
        nc.sync.dma_start(out_rows[:, :, cols(1)], result[:, :, cols(1)])
        round_half(cols(1), nc.vector.tensor_copy)
        quantise(o_words, o_scales, rounded, cols(1))
        nc.sync.dma_start(out_words[:, cols(1)], o_words[:, cols(1)].bitcast(I32))
        for q in range(4):
            queue = nc.scalar if q < 3 else nc.sync
            queue.dma_start(out_2[0, 4 * q : 4 * q + 4, :].bitcast(I32), o_scales[32 * q : 32 * q + 4, :].bitcast(I32))
